import numpy as np, ml_dtypes
CORES = [23,119,17,113]
N = 4
import mx_ref
BF = ml_dtypes.bfloat16
def decode(q):
    o = []
    for b in range(4):
        e = np.zeros((128, 128, 4), np.float32); e[np.arange(128), np.arange(128), b] = 1
        o.append(mx_ref.matmul(mx_ref.quantize(e.reshape(128, 512).astype(BF)), q))
    return np.stack(o, axis=2).reshape(128, -1)
def cut(t, i, w=512):
    return t[:, w * i:w * i + w]
def f(rng, *shape):
    return mx_ref.flush((rng.standard_normal(shape, dtype=np.float32) * np.exp2(rng.integers(-2, 3, shape[:-1] + (1,)))).astype(BF))
def wide(rng, *shape, cols=0):
    v = rng.standard_normal(shape, dtype=np.float32) * np.exp2(rng.integers(-12, 13, shape)).astype(np.float32)
    if cols: v *= np.repeat(np.exp2(rng.integers(-cols, cols + 1, shape[:-2] + (1, shape[-1] // 4))) * (rng.random(shape[:-2] + (1, shape[-1] // 4)) > 0.0625), 4, axis=-1).astype(np.float32)
    return mx_ref.flush(v.astype(BF))
T, CL, O = 512, 127, 2
def taps(v):
    d = np.zeros((N, 128, 512), BF); d[:, :, :64] = mx_ref.flush(v.astype(np.float32).astype(BF)); return d
def planted(rng, a, *v):
    d = setup_inputs(rng); d["x"] = np.array(d["x"]); t = np.zeros((N, 128, 64))
    for r in range(N):
        rows = rng.permutation(512)[:len(v)]
        for m in range(len(v)):
            p, b = divmod(int(rows[m]), 4)
            d["x"][r, p, b::4] = mx_ref.flush(a[r].astype(BF)); t[r, p, b::4] = v[m][r]
    d["u"] = taps(t); return d
def setup_inputs(rng):
    return {"x": f(rng, N, 128, 4 * T), "u": taps(f(rng, N, 128, 64).astype(np.float32) * np.float32(CL * 0.005)), "w": f(rng, N, 128, 2 * O * 512)}
def setup_inputs_edge(rng):
    a = rng.uniform(-0.25, 0.25, (N, T)); a[:, :CL] = -rng.uniform(0.75, 1.25, (N, CL)); a[:, T - CL:] = rng.uniform(0.75, 1.25, (N, CL))
    return planted(rng, a, rng.uniform(0.5, 1.0, (N, 16)) * CL)
def setup_inputs_halves(rng):
    return planted(rng, rng.choice([-3.0, -1.0, 1.0, 3.0], (N, T)), rng.choice([-2.5, -1.5, -0.5, 0.5, 1.5, 2.5], (N, 16)))
def setup_inputs_last(rng):
    a = rng.choice([-1.0, 1.0], (N, T)); a[:, 0] = -1.0; a[:, T - 1] = 1.0
    return planted(rng, a, np.full((N, 16), CL + 1.0), np.full((N, 16), -1.25))
def setup_inputs_out(rng):
    return planted(rng, np.ones((N, T)), np.tile(np.repeat([-256.0, 256.0], 8), (N, 1)))
def setup_inputs_spread(rng):
    d = setup_inputs(rng); d["x"] = wide(rng, N, 128, 4 * T, cols=8)
    d["u"] = taps(f(rng, N, 128, 64).astype(np.float32) * np.float32(CL * 0.005 * 2.0 ** -10)); return d
def check_inputs(d):
    return ["u"] if (np.asarray(d["u"])[:, :, 64:].astype(np.float32) != 0).any() else []
def reference(x, u, w):
    V = np.concatenate([decode(mx_ref.quantize(x[r])) for r in range(N)], axis=1).reshape(8, 16, N * T, 4)
    y = np.zeros((N, 128, O * T), np.float32)
    for r in range(N):
        o = mx_ref.matmul(mx_ref.quantize(u[r]), mx_ref.quantize(x[r]))[:16]
        o = np.minimum(np.maximum(o, np.float32(-CL)), np.float32(CL))
        n = np.rint(o); fr = o - n
        i = np.clip(r * T + np.arange(T) + n.astype(np.int64), 0, N * T - 1); i1 = np.minimum(i + 1, N * T - 1)
        M = []
        for k in range(2):
            t = np.zeros((8, 16, T, 4), np.float32)
            for g in range(8):
                a, b = V[g][:, i[8 * k + g]], V[g][:, i1[8 * k + g]]
                t[g] = a + fr[8 * k + g][None, :, None] * (b - a)
            M.append(mx_ref.quantize(t.reshape(128, 4 * T).astype(BF)))
        for c in range(O):
            y[r][:, T * c:T * c + T] = mx_ref.matmul(mx_ref.quantize(np.ascontiguousarray(cut(w[r], c))), M[0]) + mx_ref.matmul(mx_ref.quantize(np.ascontiguousarray(cut(w[r], O + c))), M[1])
    return {"y": y}

@@ -1,0 +1,327 @@
+from concourse.bass import DstId, RemoteDMATransfer
+from concourse.mybir import dt, AluOpType, ActivationFunctionType
+
+N, TC, CL = 4, 512, 127
+HAL = 128
+OWN, RGT, LFT = 2, 514, 642
+WIN = 770
+MAGIC = 12582912.0
+
+F32, BF, U16, I32 = "float32", "bfloat16", "uint16", "int32"
+X4 = "float8_e4m3fn_x4"
+SCRATCH = {
+    "xt": ("sbuf", [128, 4 * TC + 16], BF),
+    "us": ("sbuf", [128, 16, 4], BF),
+    "zu": ("sbuf", [128, 33, 64], BF),
+    "wt": ("sbuf", [128, 4 * TC], BF),
+    "ones": ("sbuf", [128, 128], BF),
+    "unit": ("sbuf", [128, 528], BF),
+    "pidx": ("sbuf", [128, 2], I32),
+    "pint": ("sbuf", [128, 4], I32),
+    "pflt": ("sbuf", [128, 4], F32),
+    "bas0": ("sbuf", [128, 128], I32),
+    "bas": ("sbuf", [128, 128], I32),
+    "xq": ("sbuf", [128, TC], X4), "xs": ("sbuf", [128, TC], "uint8"),
+    "xq1": ("sbuf", [128, TC], X4), "xs1": ("sbuf", [128, TC], "uint8"),
+    "zq": ("sbuf", [128, 528], X4), "zs": ("sbuf", [128, 528], "uint8"),
+    "eq": ("sbuf", [128, 512], X4), "es": ("sbuf", [128, 512], "uint8"),
+    "wq": ("sbuf", [128, 512], X4), "ws": ("sbuf", [128, 512], "uint8"),
+    "hq": ("sbuf", [128, 2 * HAL], X4), "hs": ("sbuf", [128, 2 * HAL], "uint8"),
+    "vw": ("sbuf", [128, 4 * WIN], F32),
+    "dw": ("sbuf", [128, 4 * WIN], F32),
+    "yb": ("sbuf", [128, 2 * TC], F32),
+    "ps": ("psum", [128, 4096], F32),
+}
+for _k in range(2):
+    SCRATCH.update({
+        "ni%d" % _k: ("sbuf", [128, 128], I32), "pl%d" % _k: ("sbuf", [128, 128], I32),
+        "wr%d" % _k: ("sbuf", [128, 32], I32), "ab%d" % _k: ("sbuf", [128, 128], F32),
+        "cn%d" % _k: ("sbuf", [128, 128], I32), "dp%d" % _k: ("sbuf", [128, 128], I32),
+        "vl%d" % _k: ("sbuf", [128, 128], U16), "dl%d" % _k: ("sbuf", [128, 128], U16),
+        "tm%d" % _k: ("sbuf", [128, TC], F32), "rn%d" % _k: ("sbuf", [128, TC], F32),
+        "fr%d" % _k: ("sbuf", [128, 4 * TC], F32), "pp%d" % _k: ("sbuf", [128, 4 * TC], F32),
+        "mt%d" % _k: ("sbuf", [128, 4 * TC], BF),
+        "mq%d" % _k: ("sbuf", [128, TC], X4), "ms%d" % _k: ("sbuf", [128, TC], "uint8"),
+    })
+SEMAPHORES = ["cV", "cS", "cP", "cG", "sent", "arrR", "arrL", "dx1", "dx2", "du", "dwt"] + ["dy%d" % i for i in range(6)]
+
+Op, Fn = AluOpType, ActivationFunctionType
+
+
+def scheduler(g, T):
+    queues = {"V": g.vector, "S": g.scalar, "P": g.tensor, "G": g, "Y": g.sync}
+    clock = {q: {} for q in queues}
+    done = {}
+    tick, log, scale = {}, {}, {}
+
+    def after(q, reads, writes):
+        deps = {}
+        for acc, mine in ((reads, "r"), (writes, "w")):
+            for key, lo, hi in acc:
+                for (l, h, kind, src, t, oq) in log.get(key, []):
+                    if h <= lo or hi <= l:
+                        continue
+                    bank = key[:2] == "ps"
+                    if mine == "r" and kind == "r" and not (bank and oq != q):
+                        continue
+                    if src == "c" + q and (kind == "r" or bank):
+                        continue
+                    deps[src] = max(deps.get(src, 0), t)
+        for src, t in list(deps.items()):
+            if clock[q].get(src, 0) >= t:
+                continue
+            if any(s2 != src and done[(s2, t2)].get(src, 0) >= t and clock[q].get(s2, 0) < t2 for s2, t2 in deps.items()):
+                continue
+            queues[q].wait_ge(T.sem[src], t * scale.get(src, 1))
+        for src, t in deps.items():
+            for s, v in done[(src, t)].items():
+                clock[q][s] = max(clock[q].get(s, 0), v)
+
+    def note(q, src, reads, writes):
+        tick[src] = tick.get(src, 0) + 1
+        c = dict(clock[q]) if q else {}
+        c[src] = tick[src]
+        done[(src, tick[src])] = c
+        for acc, kind in ((reads, "r"), (writes, "w")):
+            for key, lo, hi in acc:
+                log.setdefault(key, []).append((lo, hi, kind, src, tick[src], q))
+
+    def do(q, call, reads, writes):
+        after(q, reads, writes)
+        call(queues[q]).then_inc(T.sem["c" + q], 1)
+        note(q, "c" + q, reads, writes)
+
+    def dma(q, sem, out, in_, reads, writes):
+        after(q, reads, writes)
+        queues[q].dma_start(out, in_).then_inc(T.sem[sem], 16)
+        scale[sem] = 16
+        note(q, sem, reads, writes)
+
+    def arrival(sem, count, writes):
+        scale[sem] = count
+        note(None, sem, [], writes)
+
+    def drain(q):
+        for src, t in tick.items():
+            if clock[q].get(src, 0) < t:
+                queues[q].wait_ge(T.sem[src], t * scale.get(src, 1))
+
+    return do, dma, after, arrival, drain
+
+
+def rank_program(g, core, T, topo):
+    rank = T.rank_of(core)
+    if rank is None:
+        return
+    do, dma, after, arrival, drain = scheduler(g, T)
+    prev = T.cores[rank - 1] if rank > 0 else None
+    nxt = T.cores[rank + 1] if rank < N - 1 else None
+    ENG = 4
+    if nxt is not None:
+        arrival("arrR", 2 * ENG, [("hq", 0, HAL)])
+    if prev is not None:
+        arrival("arrL", 2 * ENG, [("hq", HAL, 2 * HAL)])
+
+    def quant(codes, planes, src, c0, n, e0, srckey, lo, hi, key):
+        do("V", lambda v: v.quantize_mx(T[codes][:, c0:c0 + n], T[planes][:, c0:c0 + n], src(e0, e0 + 4 * n)),
+           [(srckey, lo, hi)], [(key, c0, c0 + n)])
+
+    def mm(bank, n, ls, l0, rs, r0, start, stop):
+        names = {"zq": "zs", "xq": "xs", "xq1": "xs1", "eq": "es", "wq": "ws", "hq": "hs", "mq0": "ms0", "mq1": "ms1"}
+        do("P", lambda p: p.matmul_mx(T.ps[:, 512 * bank:512 * bank + n], T[ls][:, l0:l0 + 128], T[names[ls]][:, l0:l0 + 128],
+                                      T[rs][:, r0:r0 + n], T[names[rs]][:, r0:r0 + n], start, stop),
+           [(ls, l0, l0 + 128), (rs, r0, r0 + n)], [("ps%d" % bank, 0, 512)])
+
+    dma("Y", "dx1", T.xt[:, 0:1024], T.x[:, 0:1024], [], [("xt", 0, 256)])
+    dma("S", "du", T.us[:, :, :], T.u[:, 0:64], [], [("us", 0, 1)])
+    dma("Y", "dx2", T.xt[:, 1024:2048], T.x[:, 1024:2048], [], [("xt", 256, 512)])
+
+    do("G", lambda e: e.iota(T.pidx[:, 0:1], [[0, 1]], 0, 1), [], [("pidx", 0, 1)])
+    do("G", lambda e: e.iota(T.bas0[:], [[4, 128]], OWN, 0), [], [("bas0", 0, 1)])
+    do("V", lambda v: v.memset(T.ones[:], 1.0), [], [("ones", 0, 1)])
+    do("V", lambda v: v.memset(T.unit[:], 0.0), [], [("unit", 0, 1)])
+    do("G", lambda e: e.affine_select(T.unit[:, 3:515:4], T.ones[:], [[-1, 128]], Op.is_equal, 0.0, 0, 1),
+       [("ones", 0, 1)], [("unit", 0, 1)])
+    do("V", lambda v: v.memset(T.zu[:, 0:17, :], 0.0), [], [("zuz", 0, 1)])
+    do("V", lambda v: v.memset(T.xt[:, 2048:2064], 0.0), [], [("xt", 512, 516)])
+    do("V", lambda v: v.memset(T.vw[:, 0:8], 0.0), [], [("vw%d" % b, 0, 2) for b in range(4)])
+    do("V", lambda v: v.memset(T.dw[:, 0:8], 0.0), [], [("dw%d" % b, 0, 2) for b in range(4)])
+    if nxt is None:
+        do("V", lambda v: v.memset(T.dw[:, 4 * (RGT - 1):4 * LFT], 0.0), [], [("dw%d" % b, RGT - 1, LFT) for b in range(4)])
+        do("V", lambda v: v.memset(T.vw[:, 4 * RGT:4 * LFT], 0.0), [], [("vw%d" % b, RGT, LFT) for b in range(4)])
+    do("V", lambda v: v.tensor_scalar(T.pint[:, 0:1], T.pidx[:, 0:1], 3, None, Op.bitwise_and), [("pidx", 0, 1)], [("pint", 0, 1)])
+    do("V", lambda v: v.tensor_scalar(T.pint[:, 1:2], T.pidx[:, 0:1], 2, 3, Op.arith_shift_right, Op.bitwise_and),
+       [("pidx", 0, 1)], [("pint", 1, 2)])
+    do("V", lambda v: v.tensor_copy(T.pflt[:, 0:2], T.pint[:, 0:2]), [("pint", 0, 2)], [("pflt", 0, 1)])
+    do("V", lambda v: v.tensor_scalar(T.bas[:], T.bas0[:], T.pflt[:, 1:2], None, Op.add), [("bas0", 0, 1), ("pflt", 0, 1)], [("bas", 0, 1)])
+    for b in range(4):
+        quant("eq", "es", lambda lo, hi: T.unit[:, lo:hi], 128 * b, 128, 3 - b, "unit", 0, 1, "eq")
+
+    us = [("us", 0, 1)]
+    do("V", lambda v: v.tensor_copy(T.zu[:, 0:16, 48:52], T.us[:, :, :]), us, [("zuz", 0, 1)])
+    do("V", lambda v: v.tensor_copy(T.zu[:, 0:16, 52:56], T.us[:, :, :]), us, [("zuz", 0, 1)])
+    do("S", lambda s: s.activation(T.zu[:, 17:33, 0:4], T.us[:, :, :], Fn.Copy), us, [("zuu", 0, 4)])
+    do("S", lambda s: s.activation(T.zu[:, 17:33, 4:8], T.us[:, :, :], Fn.Copy), us, [("zuu", 4, 8)])
+    do("V", lambda v: v.tensor_copy(T.zu[:, 0:16, 56:64], T.zu[:, 0:16, 48:56]), [("zuz", 0, 1)], [("zuz", 0, 1)])
+    for w in (8, 16, 32):
+        do("S", lambda s, w=w: s.activation(T.zu[:, 17:33, w:2 * w], T.zu[:, 17:33, 0:w], Fn.Copy), [("zuu", 0, w)], [("zuu", w, 2 * w)])
+    do("V", lambda v: v.quantize_mx(T.zq[:, 0:272], T.zs[:, 0:272], T.zu[:, 0:17, :]), [("zuz", 0, 1)], [("zq", 0, 272)])
+    do("V", lambda v: v.quantize_mx(T.zq[:, 272:528], T.zs[:, 272:528], T.zu[:, 17:33, :]), [("zuu", 0, 64)], [("zq", 272, 528)])
+
+    xv = lambda lo, hi: T.xt[:, lo:hi]
+    quant("xq", "xs", xv, 0, 256, 0, "xt", 0, 256, "xq")
+    quant("xq1", "xs1", xv, 0, 254, 4, "xt", 1, 255, "xq1")
+    quant("xq", "xs", xv, 256, 256, 1024, "xt", 256, 512, "xq")
+    quant("xq1", "xs1", xv, 254, 258, 1020, "xt", 255, 513, "xq1")
+
+    sends = []
+    if prev is not None:
+        sends.append((prev, 0, 0, "arrR"))
+    if nxt is not None:
+        sends.append((nxt, TC - HAL, HAL, "arrL"))
+    after("G", [("xq", c0, c0 + HAL) for _, c0, _, _ in sends], [])
+    for plane in (0, 1):
+        tr = []
+        for i, (dst, c0, d0, sem) in enumerate(sends):
+            rid, pid, _ = topo.addr(dst)
+            eng = topo.engines(core, dst)[ENG * i:ENG * i + ENG]
+            s, d = (T.xs[:, c0:c0 + HAL], T.hs[:, d0:d0 + HAL]) if plane else \
+                (T.xq[:, c0:c0 + HAL].bitcast(dt.uint8), T.hq[:, d0:d0 + HAL].bitcast(dt.uint8))
+            tr.append(RemoteDMATransfer(dst_ids=[DstId(rid=rid, pnc=pid)], dma_engine_mask=sum(1 << e for e in eng),
+                                        remote_sem=T.sem[sem], src=s, dst=d))
+        g.remote_dma_fused(tr, local_sem=T.sem.sent)
+    sent = 2 * ENG * len(sends)
+
+    after("Y", [("xt", 0, 512)], [])
+    dma("Y", "dwt", T.wt[:], T.w[:], [], [("wt", 0, 1)])
+
+    def unpack_mm(b):
+        mm(b, TC, "eq", 128 * b, "xq", 0, True, True)
+
+    def unpack_copy(b):
+        do("S", lambda s: s.activation(T.vw[:, 4 * OWN + b:4 * RGT:4], T.ps[:, 512 * b:512 * b + 512], Fn.Copy),
+           [("ps%d" % b, 0, 512)], [("vw%d" % b, OWN, RGT)])
+
+    def diff(b):
+        do("V", lambda v: v.tensor_tensor(T.dw[:, 4 * OWN + b:4 * (RGT - 1):4], T.ps[:, 512 * b + 1:512 * b + 512],
+                                          T.vw[:, 4 * OWN + b:4 * (RGT - 1):4], Op.subtract),
+           [("ps%d" % b, 0, 512), ("vw%d" % b, OWN, RGT - 1)], [("dw%d" % b, OWN, RGT - 1)])
+
+    def offs_mm(k):
+        mm(6 + k, TC, "zq", 272 + 128 * k, "xq", 0, True, True)
+
+    def list_mm(k):
+        for a in range(4):
+            mm(4 + k, 510, "zq", 128 * k + 12 - 4 * a, "xq1" if a & 1 else "xq", a & 2, a == 0, a == 3)
+
+    def frac_n(k, j0, j1):
+        do("S", lambda s: s.activation(T["tm%d" % k][:, j0:j1], T.ps[:, 512 * (6 + k) + j0:512 * (6 + k) + j1], Fn.Copy, bias=MAGIC),
+           [("ps%d" % (6 + k), 0, 512)], [("tm%d" % k, j0, j1)])
+        do("S", lambda s: s.activation(T["rn%d" % k][:, j0:j1], T["tm%d" % k][:, j0:j1], Fn.Copy, bias=-MAGIC),
+           [("tm%d" % k, j0, j1)], [("rn%d" % k, j0, j1)])
+
+    def frac_sub(k, j0, j1):
+        do("V", lambda v: v.tensor_tensor(T["fr%d" % k][:, 4 * j0:4 * j1:4], T.ps[:, 512 * (6 + k) + j0:512 * (6 + k) + j1],
+                                          T["rn%d" % k][:, j0:j1], Op.subtract),
+           [("ps%d" % (6 + k), 0, 512), ("rn%d" % k, j0, j1)], [("fr%d0" % k, j0, j1)])
+
+    def frac_rep(k, j0, j1):
+        fr = T["fr%d" % k]
+        do("G", lambda e: e.affine_select(fr[:, 4 * j0 + 3:4 * j1:4], fr[:, 4 * j0:4 * j1:4], [[1, j1 - j0]], Op.is_gt, 0.0, 1, 0),
+           [("fr%d0" % k, j0, j1)], [("fr%d3" % k, j0, j1)])
+        for b in (1, 2):
+            do("S", lambda s, b=b: s.activation(fr[:, 4 * j0 + b:4 * j1:4], fr[:, 4 * j0:4 * j1:4], Fn.Copy),
+               [("fr%d0" % k, j0, j1)], [("fr%d%d" % (k, b), j0, j1)])
+
+    def lists(k):
+        ni, pl, wr, ab, cn, dp, vl, dl = (T[n + str(k)] for n in ("ni", "pl", "wr", "ab", "cn", "dp", "vl", "dl"))
+        key = lambda n, lo=0, hi=128: (n + str(k), lo, hi)
+        d = T.ps[:, 512 * (4 + k):512 * (4 + k) + 509:4]
+        bank = ("ps%d" % (4 + k), 0, 512)
+        do("V", lambda v: v.tensor_scalar(ni[:], d, float(-CL), float(CL), Op.max, Op.min), [bank], [key("ni")])
+        do("S", lambda s: s.activation(ab[:], d, Fn.Abs), [bank], [key("ab")])
+        do("V", lambda v: v.tensor_tensor(pl[:], ni[:], T.bas[:], Op.add), [key("ni"), ("bas", 0, 1)], [key("pl")])
+        if prev is None:
+            do("V", lambda v: v.tensor_scalar(pl[:, 0:32], pl[:, 0:32], float(OWN), None, Op.max), [key("pl", 0, 32)], [key("pl", 0, 32)])
+        else:
+            do("V", lambda v: v.tensor_scalar(wr[:], pl[:, 0:32], float(OWN), float(WIN - OWN), Op.is_lt, Op.mult), [key("pl", 0, 32)], [key("wr")])
+            do("V", lambda v: v.tensor_tensor(pl[:, 0:32], pl[:, 0:32], wr[:], Op.add), [key("pl", 0, 32), key("wr")], [key("pl", 0, 32)])
+        if nxt is None:
+            do("V", lambda v: v.tensor_scalar(pl[:, 96:128], pl[:, 96:128], float(RGT - 1), None, Op.min), [key("pl", 96, 128)], [key("pl", 96, 128)])
+        do("V", lambda v: v.tensor_scalar(cn[:], ab[:], float(CL), None, Op.is_lt), [key("ab")], [key("cn")])
+        do("V", lambda v: v.tensor_scalar(vl[:], pl[:], 4.0, T.pflt[:, 0:1], Op.mult, Op.add), [key("pl"), ("pflt", 0, 1)], [key("vl")])
+        do("V", lambda v: v.tensor_tensor(dp[:], pl[:], cn[:], Op.mult), [key("pl"), key("cn")], [key("dp")])
+        do("V", lambda v: v.tensor_scalar(dl[:], dp[:], 4.0, T.pflt[:, 0:1], Op.mult, Op.add), [key("dp"), ("pflt", 0, 1)], [key("dl")])
+
+    def slope(k, j0, j1, end):
+        do("V", lambda v: v.tensor_tensor(T["pp%d" % k][:, 4 * j0:4 * j1], T.dw[:, 0:4 * end].indirect(T["dl%d" % k][:, j0 // 4:j1 // 4]),
+                                          T["fr%d" % k][:, 4 * j0:4 * j1], Op.mult),
+           [("dw%d" % b, 0, end) for b in range(4)] + [("fr%d%d" % (k, b), j0, j1) for b in range(4)] + [("dl%d" % k, 0, 128)],
+           [("pp%d" % k, j0, j1)])
+
+    def tap(k, j0, j1, end):
+        do("V", lambda v: v.tensor_tensor(T["mt%d" % k][:, 4 * j0:4 * j1], T.vw[:, 0:4 * end].indirect(T["vl%d" % k][:, j0 // 4:j1 // 4]),
+                                          T["pp%d" % k][:, 4 * j0:4 * j1], Op.add),
+           [("vw%d" % b, 0, end) for b in range(4)] + [("pp%d" % k, j0, j1), ("vl%d" % k, 0, 128)], [("mt%d" % k, j0, j1)])
+
+    def tap_q(k, j0, j1):
+        quant("mq%d" % k, "ms%d" % k, lambda lo, hi: T["mt%d" % k][:, lo:hi], j0, j1 - j0, 4 * j0, "mt%d" % k, j0, j1, "mq%d" % k)
+
+    def out_mm(j0, j1, banks):
+        for k in range(2):
+            for o in range(2):
+                mm(banks[o], j1 - j0, "wq", 128 * (2 * k + o), "mq%d" % k, j0, k == 0, k == 1)
+
+    def out_copy(j0, j1, banks, last, n):
+        for o in range(2):
+            src, dst = T.ps[:, 512 * banks[o]:512 * banks[o] + j1 - j0], T.yb[:, TC * o + j0:TC * o + j1]
+            acc = ([("ps%d" % banks[o], 0, 512)], [("yb%d" % o, j0, j1)])
+            if last and o == 1:
+                do("V", lambda v: v.tensor_copy(dst, src), *acc)
+            else:
+                do("S", lambda s: s.activation(dst, src, Fn.Copy), *acc)
+            dma("S" if last and o == 1 else "Y", "dy%d" % (2 * n + o), T.y[:, TC * o + j0:TC * o + j1], dst, [("yb%d" % o, j0, j1)], [])
+
+    A = (128, 384)
+    unpack_mm(0); unpack_mm(1); offs_mm(0); list_mm(0); unpack_mm(2); unpack_mm(3); offs_mm(1); list_mm(1)
+    unpack_copy(0); unpack_copy(1); frac_n(0, *A)
+    diff(0); diff(1); frac_sub(0, *A); frac_rep(0, *A)
+    lists(0)
+    unpack_copy(2); unpack_copy(3)
+    diff(2); diff(3)
+    slope(0, *A, RGT - 1)
+    frac_n(1, 0, TC); lists(1); frac_sub(1, 0, TC); frac_rep(1, 0, TC)
+    tap(0, *A, RGT)
+    slope(1, *A, RGT - 1)
+    quant("wq", "ws", lambda lo, hi: T.wt[:, lo:hi], 0, 512, 0, "wt", 0, 1, "wq")
+    tap(1, *A, RGT)
+    for j in ((0, 128), (384, 512)):
+        frac_n(0, *j); frac_sub(0, *j); frac_rep(0, *j)
+    tap_q(0, *A); tap_q(1, *A)
+    h0, h1 = (0 if nxt is not None else HAL), (2 * HAL if prev is not None else HAL)
+    w0, w1 = RGT + h0, RGT + h1
+    for b in range(4):
+        mm(b, h1 - h0, "eq", 128 * b, "hq", h0, True, True)
+    out_mm(*A, (4, 5))
+    for b in range(4):
+        do("S", lambda s: s.activation(T.vw[:, 4 * w0 + b:4 * w1:4], T.ps[:, 512 * b:512 * b + w1 - w0], Fn.Copy),
+           [("ps%d" % b, 0, 512)], [("vw%d" % b, w0, w1)])
+        e = 1 if nxt is None else 0
+        do("V", lambda v: v.tensor_tensor(T.dw[:, 4 * (w0 - 1 + e) + b:4 * (w1 - 1):4], T.ps[:, 512 * b + e:512 * b + w1 - w0],
+                                          T.vw[:, 4 * (w0 - 1 + e) + b:4 * (w1 - 1):4], Op.subtract),
+           [("ps%d" % b, 0, 512), ("vw%d" % b, w0 - 1 + e, w1 - 1)], [("dw%d" % b, w0 - 1 + e, w1 - 1)])
+    if prev is not None:
+        do("V", lambda v: v.tensor_tensor(T.dw[:, 4 * (WIN - 1):4 * WIN], T.vw[:, 4 * OWN:4 * OWN + 4], T.vw[:, 4 * (WIN - 1):4 * WIN], Op.subtract),
+           [("vw%d" % b, OWN, OWN + 1) for b in range(4)] + [("vw%d" % b, WIN - 1, WIN) for b in range(4)],
+           [("dw%d" % b, WIN - 1, WIN) for b in range(4)])
+    out_copy(*A, (4, 5), False, 0)
+    L = (0, 128, RGT - 1 if prev is None else WIN, RGT if prev is None else WIN)
+    R = (384, 512, LFT - 1 if nxt is not None else RGT, LFT if nxt is not None else RGT)
+    for n, (j0, j1, de, ve), banks in ((1, L if prev is None else R, (6, 7)), (2, R if prev is None else L, (0, 1))):
+        slope(0, j0, j1, de); slope(1, j0, j1, de)
+        tap(0, j0, j1, ve); tap(1, j0, j1, ve)
+        tap_q(0, j0, j1); tap_q(1, j0, j1)
+        out_mm(j0, j1, banks)
+        out_copy(j0, j1, banks, n == 2, n)
+    g.wait_ge(T.sem.sent, sent)
+    drain("Y")

@@ -36,14 +36,15 @@ for _k in range(2):
     SCRATCH.update({
         "ni%d" % _k: ("sbuf", [128, 128], I32), "pl%d" % _k: ("sbuf", [128, 128], I32),
         "wr%d" % _k: ("sbuf", [128, 32], I32), "ab%d" % _k: ("sbuf", [128, 128], F32),
-        "cn%d" % _k: ("sbuf", [128, 128], I32), "dp%d" % _k: ("sbuf", [128, 128], I32),
+        "sg%d" % _k: ("sbuf", [128, 128], F32), "dp%d" % _k: ("sbuf", [128, 128], I32),
         "vl%d" % _k: ("sbuf", [128, 128], U16), "dl%d" % _k: ("sbuf", [128, 128], U16),
         "tm%d" % _k: ("sbuf", [128, TC], F32), "rn%d" % _k: ("sbuf", [128, TC], F32),
         "fr%d" % _k: ("sbuf", [128, 4 * TC], F32), "pp%d" % _k: ("sbuf", [128, 4 * TC], F32),
         "mt%d" % _k: ("sbuf", [128, 4 * TC], BF),
         "mq%d" % _k: ("sbuf", [128, TC], X4), "ms%d" % _k: ("sbuf", [128, TC], "uint8"),
     })
-SEMAPHORES = ["cV", "cS", "cP", "cG", "sent", "arrR", "arrL", "dx1", "dx2", "du", "dwt"] + ["dy%d" % i for i in range(6)]
+SEMAPHORES = ["cV", "cS", "cP", "cG", "sent", "arrR", "arrL", "dx1", "dx2", "du", "dwt"] + \
+    ["dy%d" % i for i in range(6)] + ["da%d" % i for i in range(3)]
 
 Op, Fn = AluOpType, ActivationFunctionType
 
@@ -91,9 +92,9 @@ def scheduler(g, T):
         call(queues[q]).then_inc(T.sem["c" + q], 1)
         note(q, "c" + q, reads, writes)
 
-    def dma(q, sem, out, in_, reads, writes):
+    def dma(q, sem, out, in_, reads, writes, **kw):
         after(q, reads, writes)
-        queues[q].dma_start(out, in_).then_inc(T.sem[sem], 16)
+        queues[q].dma_start(out, in_, **kw).then_inc(T.sem[sem], 16)
         scale[sem] = 16
         note(q, sem, reads, writes)
 
@@ -122,12 +123,13 @@ def rank_program(g, core, T, topo):
     if prev is not None:
         arrival("arrL", 2 * ENG, [("hq", HAL, 2 * HAL)])
 
-    def quant(codes, planes, src, c0, n, e0, srckey, lo, hi, key):
-        do("V", lambda v: v.quantize_mx(T[codes][:, c0:c0 + n], T[planes][:, c0:c0 + n], src(e0, e0 + 4 * n)),
-           [(srckey, lo, hi)], [(key, c0, c0 + n)])
+    def quant(codes, planes, buf, c0, n, e0, lo, hi, srckey=None):
+        do("V", lambda v: v.quantize_mx(T[codes][:, c0:c0 + n], T[planes][:, c0:c0 + n], T[buf][:, e0:e0 + 4 * n]),
+           [(srckey or buf, lo, hi)], [(codes, c0, c0 + n)])
+
+    names = {"zq": "zs", "xq": "xs", "xq1": "xs1", "eq": "es", "wq": "ws", "hq": "hs", "mq0": "ms0", "mq1": "ms1"}
 
     def mm(bank, n, ls, l0, rs, r0, start, stop):
-        names = {"zq": "zs", "xq": "xs", "xq1": "xs1", "eq": "es", "wq": "ws", "hq": "hs", "mq0": "ms0", "mq1": "ms1"}
         do("P", lambda p: p.matmul_mx(T.ps[:, 512 * bank:512 * bank + n], T[ls][:, l0:l0 + 128], T[names[ls]][:, l0:l0 + 128],
                                       T[rs][:, r0:r0 + n], T[names[rs]][:, r0:r0 + n], start, stop),
            [(ls, l0, l0 + 128), (rs, r0, r0 + n)], [("ps%d" % bank, 0, 512)])
@@ -154,8 +156,11 @@ def rank_program(g, core, T, topo):
        [("pidx", 0, 1)], [("pint", 1, 2)])
     do("V", lambda v: v.tensor_copy(T.pflt[:, 0:2], T.pint[:, 0:2]), [("pint", 0, 2)], [("pflt", 0, 1)])
     do("V", lambda v: v.tensor_scalar(T.bas[:], T.bas0[:], T.pflt[:, 1:2], None, Op.add), [("bas0", 0, 1), ("pflt", 0, 1)], [("bas", 0, 1)])
-    for b in range(4):
-        quant("eq", "es", lambda lo, hi: T.unit[:, lo:hi], 128 * b, 128, 3 - b, "unit", 0, 1, "eq")
+
+    def unit_q(b):
+        quant("eq", "es", "unit", 128 * b, 128, 3 - b, 0, 1)
+
+    unit_q(0); unit_q(1)
 
     us = [("us", 0, 1)]
     do("V", lambda v: v.tensor_copy(T.zu[:, 0:16, 48:52], T.us[:, :, :]), us, [("zuz", 0, 1)])
@@ -164,15 +169,14 @@ def rank_program(g, core, T, topo):
     do("S", lambda s: s.activation(T.zu[:, 17:33, 4:8], T.us[:, :, :], Fn.Copy), us, [("zuu", 4, 8)])
     do("V", lambda v: v.tensor_copy(T.zu[:, 0:16, 56:64], T.zu[:, 0:16, 48:56]), [("zuz", 0, 1)], [("zuz", 0, 1)])
     for w in (8, 16, 32):
-        do("S", lambda s, w=w: s.activation(T.zu[:, 17:33, w:2 * w], T.zu[:, 17:33, 0:w], Fn.Copy), [("zuu", 0, w)], [("zuu", w, 2 * w)])
+        do("S", lambda s: s.activation(T.zu[:, 17:33, w:2 * w], T.zu[:, 17:33, 0:w], Fn.Copy), [("zuu", 0, w)], [("zuu", w, 2 * w)])
     do("V", lambda v: v.quantize_mx(T.zq[:, 0:272], T.zs[:, 0:272], T.zu[:, 0:17, :]), [("zuz", 0, 1)], [("zq", 0, 272)])
-    do("V", lambda v: v.quantize_mx(T.zq[:, 272:528], T.zs[:, 272:528], T.zu[:, 17:33, :]), [("zuu", 0, 64)], [("zq", 272, 528)])
 
-    xv = lambda lo, hi: T.xt[:, lo:hi]
-    quant("xq", "xs", xv, 0, 256, 0, "xt", 0, 256, "xq")
-    quant("xq1", "xs1", xv, 0, 254, 4, "xt", 1, 255, "xq1")
-    quant("xq", "xs", xv, 256, 256, 1024, "xt", 256, 512, "xq")
-    quant("xq1", "xs1", xv, 254, 258, 1020, "xt", 255, 513, "xq1")
+    quant("xq", "xs", "xt", 0, 256, 0, 0, 256)
+    quant("xq", "xs", "xt", 256, 256, 1024, 256, 512)
+    quant("xq1", "xs1", "xt", 0, 254, 4, 1, 255)
+    quant("xq1", "xs1", "xt", 254, 258, 1020, 255, 513)
+    do("V", lambda v: v.quantize_mx(T.zq[:, 272:528], T.zs[:, 272:528], T.zu[:, 17:33, :]), [("zuu", 0, 64)], [("zq", 272, 528)])
 
     sends = []
     if prev is not None:
@@ -211,8 +215,8 @@ def rank_program(g, core, T, topo):
         mm(6 + k, TC, "zq", 272 + 128 * k, "xq", 0, True, True)
 
     def list_mm(k):
-        for a in range(4):
-            mm(4 + k, 510, "zq", 128 * k + 12 - 4 * a, "xq1" if a & 1 else "xq", a & 2, a == 0, a == 3)
+        for n, a in enumerate((0, 2, 1, 3)):
+            mm(4 + k, 510, "zq", 128 * k + 12 - 4 * a, "xq1" if a % 2 else "xq", a - a % 2, n == 0, n == 3)
 
     def frac_n(k, j0, j1):
         do("S", lambda s: s.activation(T["tm%d" % k][:, j0:j1], T.ps[:, 512 * (6 + k) + j0:512 * (6 + k) + j1], Fn.Copy, bias=MAGIC),
@@ -225,21 +229,27 @@ def rank_program(g, core, T, topo):
                                           T["rn%d" % k][:, j0:j1], Op.subtract),
            [("ps%d" % (6 + k), 0, 512), ("rn%d" % k, j0, j1)], [("fr%d0" % k, j0, j1)])
 
-    def frac_rep(k, j0, j1):
+    def frac_g(k, j0, j1):
         fr = T["fr%d" % k]
         do("G", lambda e: e.affine_select(fr[:, 4 * j0 + 3:4 * j1:4], fr[:, 4 * j0:4 * j1:4], [[1, j1 - j0]], Op.is_gt, 0.0, 1, 0),
            [("fr%d0" % k, j0, j1)], [("fr%d3" % k, j0, j1)])
+
+    def frac_s(k, j0, j1):
+        fr = T["fr%d" % k]
         for b in (1, 2):
-            do("S", lambda s, b=b: s.activation(fr[:, 4 * j0 + b:4 * j1:4], fr[:, 4 * j0:4 * j1:4], Fn.Copy),
+            do("S", lambda s: s.activation(fr[:, 4 * j0 + b:4 * j1:4], fr[:, 4 * j0:4 * j1:4], Fn.Copy),
                [("fr%d0" % k, j0, j1)], [("fr%d%d" % (k, b), j0, j1)])
 
+    def inside(k):
+        ab, sg = T["ab%d" % k], T["sg%d" % k]
+        do("S", lambda s: s.activation(ab[:], T.ps[:, 512 * (4 + k):512 * (4 + k) + 509:4], Fn.Abs), [("ps%d" % (4 + k), 0, 512)], [("ab%d" % k, 0, 128)])
+        do("S", lambda s: s.activation(sg[:], ab[:], Fn.Sign, bias=float(CL), scale=-1.0), [("ab%d" % k, 0, 128)], [("sg%d" % k, 0, 128)])
+
     def lists(k):
-        ni, pl, wr, ab, cn, dp, vl, dl = (T[n + str(k)] for n in ("ni", "pl", "wr", "ab", "cn", "dp", "vl", "dl"))
+        ni, pl, wr, sg, dp, vl, dl = (T[n + str(k)] for n in ("ni", "pl", "wr", "sg", "dp", "vl", "dl"))
         key = lambda n, lo=0, hi=128: (n + str(k), lo, hi)
         d = T.ps[:, 512 * (4 + k):512 * (4 + k) + 509:4]
-        bank = ("ps%d" % (4 + k), 0, 512)
-        do("V", lambda v: v.tensor_scalar(ni[:], d, float(-CL), float(CL), Op.max, Op.min), [bank], [key("ni")])
-        do("S", lambda s: s.activation(ab[:], d, Fn.Abs), [bank], [key("ab")])
+        do("V", lambda v: v.tensor_scalar(ni[:], d, float(-CL), float(CL), Op.max, Op.min), [("ps%d" % (4 + k), 0, 512)], [key("ni")])
         do("V", lambda v: v.tensor_tensor(pl[:], ni[:], T.bas[:], Op.add), [key("ni"), ("bas", 0, 1)], [key("pl")])
         if prev is None:
             do("V", lambda v: v.tensor_scalar(pl[:, 0:32], pl[:, 0:32], float(OWN), None, Op.max), [key("pl", 0, 32)], [key("pl", 0, 32)])
@@ -248,9 +258,8 @@ def rank_program(g, core, T, topo):
             do("V", lambda v: v.tensor_tensor(pl[:, 0:32], pl[:, 0:32], wr[:], Op.add), [key("pl", 0, 32), key("wr")], [key("pl", 0, 32)])
         if nxt is None:
             do("V", lambda v: v.tensor_scalar(pl[:, 96:128], pl[:, 96:128], float(RGT - 1), None, Op.min), [key("pl", 96, 128)], [key("pl", 96, 128)])
-        do("V", lambda v: v.tensor_scalar(cn[:], ab[:], float(CL), None, Op.is_lt), [key("ab")], [key("cn")])
         do("V", lambda v: v.tensor_scalar(vl[:], pl[:], 4.0, T.pflt[:, 0:1], Op.mult, Op.add), [key("pl"), ("pflt", 0, 1)], [key("vl")])
-        do("V", lambda v: v.tensor_tensor(dp[:], pl[:], cn[:], Op.mult), [key("pl"), key("cn")], [key("dp")])
+        do("V", lambda v: v.tensor_tensor(dp[:], pl[:], sg[:], Op.mult), [key("pl"), key("sg")], [key("dp")])
         do("V", lambda v: v.tensor_scalar(dl[:], dp[:], 4.0, T.pflt[:, 0:1], Op.mult, Op.add), [key("dp"), ("pflt", 0, 1)], [key("dl")])
 
     def slope(k, j0, j1, end):
@@ -264,15 +273,22 @@ def rank_program(g, core, T, topo):
                                           T["pp%d" % k][:, 4 * j0:4 * j1], Op.add),
            [("vw%d" % b, 0, end) for b in range(4)] + [("pp%d" % k, j0, j1), ("vl%d" % k, 0, 128)], [("mt%d" % k, j0, j1)])
 
-    def tap_q(k, j0, j1):
-        quant("mq%d" % k, "ms%d" % k, lambda lo, hi: T["mt%d" % k][:, lo:hi], j0, j1 - j0, 4 * j0, "mt%d" % k, j0, j1, "mq%d" % k)
+    def far_v(k, j0, j1, end):
+        do("S", lambda s: s.activation(T["mt%d" % k][:, 4 * j0:4 * j1], T.vw[:, 0:4 * end].indirect(T["vl%d" % k][:, j0 // 4:j1 // 4]), Fn.Copy),
+           [("vw%d" % b, 0, end) for b in range(4)] + [("vl%d" % k, 0, 128)], [("mt%d" % k, j0, j1)])
 
-    def out_mm(j0, j1, banks):
+    def far_add(k, j0, j1, sem):
+        dma("G", sem, T["mt%d" % k][:, 4 * j0:4 * j1], T["pp%d" % k][:, 4 * j0:4 * j1],
+            [("pp%d" % k, j0, j1), ("mt%d" % k, j0, j1)], [("mt%d" % k, j0, j1)], accum_op=Op.add)
+
+    def tap_q(j0, j1):
+        for k in range(2):
+            quant("mq%d" % k, "ms%d" % k, "mt%d" % k, j0, j1 - j0, 4 * j0, j0, j1)
+
+    def out(j0, j1, banks, n, last=False):
         for k in range(2):
             for o in range(2):
                 mm(banks[o], j1 - j0, "wq", 128 * (2 * k + o), "mq%d" % k, j0, k == 0, k == 1)
-
-    def out_copy(j0, j1, banks, last, n):
         for o in range(2):
             src, dst = T.ps[:, 512 * banks[o]:512 * banks[o] + j1 - j0], T.yb[:, TC * o + j0:TC * o + j1]
             acc = ([("ps%d" % banks[o], 0, 512)], [("yb%d" % o, j0, j1)])
@@ -282,31 +298,37 @@ def rank_program(g, core, T, topo):
                 do("S", lambda s: s.activation(dst, src, Fn.Copy), *acc)
             dma("S" if last and o == 1 else "Y", "dy%d" % (2 * n + o), T.y[:, TC * o + j0:TC * o + j1], dst, [("yb%d" % o, j0, j1)], [])
 
-    A = (128, 384)
-    unpack_mm(0); unpack_mm(1); offs_mm(0); list_mm(0); unpack_mm(2); unpack_mm(3); offs_mm(1); list_mm(1)
-    unpack_copy(0); unpack_copy(1); frac_n(0, *A)
-    diff(0); diff(1); frac_sub(0, *A); frac_rep(0, *A)
-    lists(0)
-    unpack_copy(2); unpack_copy(3)
+    A, LO, HI = (128, 384), (0, 128), (384, 512)
+    unpack_mm(0); unpack_mm(1); offs_mm(0); list_mm(0)
+    unpack_copy(0); unpack_copy(1)
+    frac_n(0, *A); frac_n(0, *LO); frac_n(0, *HI)
+    diff(0); diff(1); frac_sub(0, *A); frac_g(0, *A); frac_s(0, *A)
+    unit_q(2); unit_q(3)
+    unpack_mm(2); unpack_mm(3); offs_mm(1); list_mm(1)
+    frac_sub(0, *LO); frac_sub(0, *HI); frac_g(0, *LO); frac_g(0, *HI)
+    inside(0); unpack_copy(2); unpack_copy(3); lists(0)
     diff(2); diff(3)
+    frac_n(1, 0, TC)
     slope(0, *A, RGT - 1)
-    frac_n(1, 0, TC); lists(1); frac_sub(1, 0, TC); frac_rep(1, 0, TC)
-    tap(0, *A, RGT)
+    far_v(0, *A, RGT)
+    frac_sub(1, 0, TC)
+    inside(1)
+    frac_g(1, *A); frac_s(1, *A); frac_g(1, *LO); frac_g(1, *HI)
+    far_add(0, *A, "da0")
+    lists(1)
     slope(1, *A, RGT - 1)
-    quant("wq", "ws", lambda lo, hi: T.wt[:, lo:hi], 0, 512, 0, "wt", 0, 1, "wq")
-    tap(1, *A, RGT)
-    for j in ((0, 128), (384, 512)):
-        frac_n(0, *j); frac_sub(0, *j); frac_rep(0, *j)
-    tap_q(0, *A); tap_q(1, *A)
+    for j in (LO, HI):
+        frac_s(0, *j); frac_s(1, *j)
+    quant("wq", "ws", "wt", 0, 512, 0, 0, 1)
+
     h0, h1 = (0 if nxt is not None else HAL), (2 * HAL if prev is not None else HAL)
     w0, w1 = RGT + h0, RGT + h1
+    e = 1 if nxt is None else 0
     for b in range(4):
         mm(b, h1 - h0, "eq", 128 * b, "hq", h0, True, True)
-    out_mm(*A, (4, 5))
     for b in range(4):
         do("S", lambda s: s.activation(T.vw[:, 4 * w0 + b:4 * w1:4], T.ps[:, 512 * b:512 * b + w1 - w0], Fn.Copy),
            [("ps%d" % b, 0, 512)], [("vw%d" % b, w0, w1)])
-        e = 1 if nxt is None else 0
         do("V", lambda v: v.tensor_tensor(T.dw[:, 4 * (w0 - 1 + e) + b:4 * (w1 - 1):4], T.ps[:, 512 * b + e:512 * b + w1 - w0],
                                           T.vw[:, 4 * (w0 - 1 + e) + b:4 * (w1 - 1):4], Op.subtract),
            [("ps%d" % b, 0, 512), ("vw%d" % b, w0 - 1 + e, w1 - 1)], [("dw%d" % b, w0 - 1 + e, w1 - 1)])
@@ -314,14 +336,18 @@ def rank_program(g, core, T, topo):
         do("V", lambda v: v.tensor_tensor(T.dw[:, 4 * (WIN - 1):4 * WIN], T.vw[:, 4 * OWN:4 * OWN + 4], T.vw[:, 4 * (WIN - 1):4 * WIN], Op.subtract),
            [("vw%d" % b, OWN, OWN + 1) for b in range(4)] + [("vw%d" % b, WIN - 1, WIN) for b in range(4)],
            [("dw%d" % b, WIN - 1, WIN) for b in range(4)])
-    out_copy(*A, (4, 5), False, 0)
-    L = (0, 128, RGT - 1 if prev is None else WIN, RGT if prev is None else WIN)
-    R = (384, 512, LFT - 1 if nxt is not None else RGT, LFT if nxt is not None else RGT)
-    for n, (j0, j1, de, ve), banks in ((1, L if prev is None else R, (6, 7)), (2, R if prev is None else L, (0, 1))):
-        slope(0, j0, j1, de); slope(1, j0, j1, de)
-        tap(0, j0, j1, ve); tap(1, j0, j1, ve)
-        tap_q(0, j0, j1); tap_q(1, j0, j1)
-        out_mm(j0, j1, banks)
-        out_copy(j0, j1, banks, n == 2, n)
+    far_v(1, *A, RGT); far_add(1, *A, "da1")
+
+    L = LO + ((RGT - 1, RGT) if prev is None else (WIN, WIN))
+    R = HI + ((LFT - 1, LFT) if nxt is not None else (RGT, RGT))
+    E1, E2 = (L, R) if prev is None else (R, L)
+    slope(0, *E2[:3]); far_v(0, *E2[:2], E2[3]); far_add(0, *E2[:2], "da2")
+    slope(0, *E1[:3]); slope(1, *E1[:3])
+    tap(0, *E1[:2], E1[3]); tap(1, *E1[:2], E1[3])
+    tap_q(*E1[:2]); out(*E1[:2], (6, 7), 1)
+    slope(1, *E2[:3])
+    tap_q(*A); out(*A, (4, 5), 0)
+    tap(1, *E2[:2], E2[3])
+    tap_q(*E2[:2]); out(*E2[:2], (0, 1), 2, last=True)
     g.wait_ge(T.sem.sent, sent)
     drain("Y")

@@ -44,7 +44,7 @@ for _k in range(2):
         "mq%d" % _k: ("sbuf", [128, TC], X4), "ms%d" % _k: ("sbuf", [128, TC], "uint8"),
     })
 SEMAPHORES = ["cV", "cS", "cP", "cG", "sent", "arrR", "arrL", "dx1", "dx2", "du", "dwt"] + \
-    ["dy%d" % i for i in range(6)] + ["da%d" % i for i in range(3)]
+    ["dy%d" % i for i in range(6)] + ["da%d" % i for i in range(4)]
 
 Op, Fn = AluOpType, ActivationFunctionType
 
@@ -123,9 +123,9 @@ def rank_program(g, core, T, topo):
     if prev is not None:
         arrival("arrL", 2 * ENG, [("hq", HAL, 2 * HAL)])
 
-    def quant(codes, planes, buf, c0, n, e0, lo, hi, srckey=None):
+    def quant(codes, planes, buf, c0, n, e0, lo, hi):
         do("V", lambda v: v.quantize_mx(T[codes][:, c0:c0 + n], T[planes][:, c0:c0 + n], T[buf][:, e0:e0 + 4 * n]),
-           [(srckey or buf, lo, hi)], [(codes, c0, c0 + n)])
+           [(buf, lo, hi)], [(codes, c0, c0 + n)])
 
     names = {"zq": "zs", "xq": "xs", "xq1": "xs1", "eq": "es", "wq": "ws", "hq": "hs", "mq0": "ms0", "mq1": "ms1"}
 
@@ -149,8 +149,9 @@ def rank_program(g, core, T, topo):
     do("V", lambda v: v.memset(T.vw[:, 0:8], 0.0), [], [("vw%d" % b, 0, 2) for b in range(4)])
     do("V", lambda v: v.memset(T.dw[:, 0:8], 0.0), [], [("dw%d" % b, 0, 2) for b in range(4)])
     if nxt is None:
-        do("V", lambda v: v.memset(T.dw[:, 4 * (RGT - 1):4 * LFT], 0.0), [], [("dw%d" % b, RGT - 1, LFT) for b in range(4)])
-        do("V", lambda v: v.memset(T.vw[:, 4 * RGT:4 * LFT], 0.0), [], [("vw%d" % b, RGT, LFT) for b in range(4)])
+        for w, lo in (("dw", RGT - 1), ("vw", RGT)):
+            do("G", lambda e: e.iota(T[w][:, 4 * lo:4 * LFT], [[0, 4 * (LFT - lo)]], 0, 0, allow_small_or_imprecise_dtypes=True),
+               [], [("%s%d" % (w, b), lo, LFT) for b in range(4)])
     do("V", lambda v: v.tensor_scalar(T.pint[:, 0:1], T.pidx[:, 0:1], 3, None, Op.bitwise_and), [("pidx", 0, 1)], [("pint", 0, 1)])
     do("V", lambda v: v.tensor_scalar(T.pint[:, 1:2], T.pidx[:, 0:1], 2, 3, Op.arith_shift_right, Op.bitwise_and),
        [("pidx", 0, 1)], [("pint", 1, 2)])
@@ -229,16 +230,12 @@ def rank_program(g, core, T, topo):
                                           T["rn%d" % k][:, j0:j1], Op.subtract),
            [("ps%d" % (6 + k), 0, 512), ("rn%d" % k, j0, j1)], [("fr%d0" % k, j0, j1)])
 
-    def frac_g(k, j0, j1):
-        fr = T["fr%d" % k]
-        do("G", lambda e: e.affine_select(fr[:, 4 * j0 + 3:4 * j1:4], fr[:, 4 * j0:4 * j1:4], [[1, j1 - j0]], Op.is_gt, 0.0, 1, 0),
-           [("fr%d0" % k, j0, j1)], [("fr%d3" % k, j0, j1)])
-
-    def frac_s(k, j0, j1):
-        fr = T["fr%d" % k]
-        for b in (1, 2):
-            do("S", lambda s: s.activation(fr[:, 4 * j0 + b:4 * j1:4], fr[:, 4 * j0:4 * j1:4], Fn.Copy),
-               [("fr%d0" % k, j0, j1)], [("fr%d%d" % (k, b), j0, j1)])
+    def frac_rep(q, k, j0, j1, bs):
+        for b in bs:
+            out, in_ = T["fr%d" % k][:, 4 * j0 + b:4 * j1:4], T["fr%d" % k][:, 4 * j0:4 * j1:4]
+            call = {"S": lambda s: s.activation(out, in_, Fn.Copy), "V": lambda v: v.tensor_copy(out, in_),
+                    "G": lambda e: e.affine_select(out, in_, [[1, j1 - j0]], Op.is_gt, 0.0, 1, 0)}[q]
+            do(q, call, [("fr%d0" % k, j0, j1)], [("fr%d%d" % (k, b), j0, j1)])
 
     def inside(k):
         ab, sg = T["ab%d" % k], T["sg%d" % k]
@@ -281,14 +278,11 @@ def rank_program(g, core, T, topo):
         dma("G", sem, T["mt%d" % k][:, 4 * j0:4 * j1], T["pp%d" % k][:, 4 * j0:4 * j1],
             [("pp%d" % k, j0, j1), ("mt%d" % k, j0, j1)], [("mt%d" % k, j0, j1)], accum_op=Op.add)
 
-    def tap_q(j0, j1):
-        for k in range(2):
+    def finish(j0, j1, banks, n, first=0, last=False):
+        for k in (first, 1 - first):
             quant("mq%d" % k, "ms%d" % k, "mt%d" % k, j0, j1 - j0, 4 * j0, j0, j1)
-
-    def out(j0, j1, banks, n, last=False):
-        for k in range(2):
             for o in range(2):
-                mm(banks[o], j1 - j0, "wq", 128 * (2 * k + o), "mq%d" % k, j0, k == 0, k == 1)
+                mm(banks[o], j1 - j0, "wq", 128 * (2 * k + o), "mq%d" % k, j0, k == first, k != first)
         for o in range(2):
             src, dst = T.ps[:, 512 * banks[o]:512 * banks[o] + j1 - j0], T.yb[:, TC * o + j0:TC * o + j1]
             acc = ([("ps%d" % banks[o], 0, 512)], [("yb%d" % o, j0, j1)])
@@ -302,10 +296,10 @@ def rank_program(g, core, T, topo):
     unpack_mm(0); unpack_mm(1); offs_mm(0); list_mm(0)
     unpack_copy(0); unpack_copy(1)
     frac_n(0, *A); frac_n(0, *LO); frac_n(0, *HI)
-    diff(0); diff(1); frac_sub(0, *A); frac_g(0, *A); frac_s(0, *A)
+    diff(0); diff(1); frac_sub(0, *A); frac_rep("S", 0, *A, (1, 2)); frac_rep("V", 0, *A, (3,))
     unit_q(2); unit_q(3)
     unpack_mm(2); unpack_mm(3); offs_mm(1); list_mm(1)
-    frac_sub(0, *LO); frac_sub(0, *HI); frac_g(0, *LO); frac_g(0, *HI)
+    frac_sub(0, *LO); frac_sub(0, *HI); frac_rep("G", 0, *LO, (2, 3)); frac_rep("G", 0, *HI, (2, 3))
     inside(0); unpack_copy(2); unpack_copy(3); lists(0)
     diff(2); diff(3)
     frac_n(1, 0, TC)
@@ -313,13 +307,12 @@ def rank_program(g, core, T, topo):
     far_v(0, *A, RGT)
     frac_sub(1, 0, TC)
     inside(1)
-    frac_g(1, *A); frac_s(1, *A); frac_g(1, *LO); frac_g(1, *HI)
+    frac_rep("G", 1, *A, (3,)); frac_rep("S", 1, *A, (1, 2))
     far_add(0, *A, "da0")
+    frac_rep("G", 1, *LO, (3,)); frac_rep("G", 1, *HI, (3,))
     lists(1)
     slope(1, *A, RGT - 1)
-    for j in (LO, HI):
-        frac_s(0, *j); frac_s(1, *j)
-    quant("wq", "ws", "wt", 0, 512, 0, 0, 1)
+    far_v(1, *A, RGT); far_add(1, *A, "da1")
 
     h0, h1 = (0 if nxt is not None else HAL), (2 * HAL if prev is not None else HAL)
     w0, w1 = RGT + h0, RGT + h1
@@ -336,18 +329,19 @@ def rank_program(g, core, T, topo):
         do("V", lambda v: v.tensor_tensor(T.dw[:, 4 * (WIN - 1):4 * WIN], T.vw[:, 4 * OWN:4 * OWN + 4], T.vw[:, 4 * (WIN - 1):4 * WIN], Op.subtract),
            [("vw%d" % b, OWN, OWN + 1) for b in range(4)] + [("vw%d" % b, WIN - 1, WIN) for b in range(4)],
            [("dw%d" % b, WIN - 1, WIN) for b in range(4)])
-    far_v(1, *A, RGT); far_add(1, *A, "da1")
+    frac_rep("S", 0, *LO, (1,)); frac_rep("S", 0, *HI, (1,)); frac_rep("S", 1, *LO, (1, 2)); frac_rep("S", 1, *HI, (1, 2))
 
     L = LO + ((RGT - 1, RGT) if prev is None else (WIN, WIN))
     R = HI + ((LFT - 1, LFT) if nxt is not None else (RGT, RGT))
     E1, E2 = (L, R) if prev is None else (R, L)
-    slope(0, *E2[:3]); far_v(0, *E2[:2], E2[3]); far_add(0, *E2[:2], "da2")
-    slope(0, *E1[:3]); slope(1, *E1[:3])
-    tap(0, *E1[:2], E1[3]); tap(1, *E1[:2], E1[3])
-    tap_q(*E1[:2]); out(*E1[:2], (6, 7), 1)
-    slope(1, *E2[:3])
-    tap_q(*A); out(*A, (4, 5), 0)
+    slope(0, *E1[:3]); far_v(0, *E1[:2], E1[3]); far_add(0, *E1[:2], "da2")
+    slope(0, *E2[:3]); far_v(0, *E2[:2], E2[3]); far_add(0, *E2[:2], "da3")
+    slope(1, *E1[:3]); slope(1, *E2[:3])
+    tap(1, *E1[:2], E1[3])
+    quant("wq", "ws", "wt", 0, 512, 0, 0, 1)
+    finish(*A, (4, 5), 0)
+    finish(*E1[:2], (6, 7), 1)
     tap(1, *E2[:2], E2[3])
-    tap_q(*E2[:2]); out(*E2[:2], (0, 1), 2, last=True)
+    finish(*E2[:2], (0, 1), 2, first=1, last=True)
     g.wait_ge(T.sem.sent, sent)
     drain("Y")

from concourse.bass import DstId, RemoteDMATransfer
from concourse.mybir import dt, AluOpType, ActivationFunctionType

N, TC, CL = 4, 512, 127
HAL = 128
OWN, RGT, LFT = 2, 514, 642
WIN = 770
MAGIC = 12582912.0

F32, BF, U16, I32 = "float32", "bfloat16", "uint16", "int32"
X4 = "float8_e4m3fn_x4"
SCRATCH = {
    "xt": ("sbuf", [128, 4 * TC + 16], BF),
    "us": ("sbuf", [128, 16, 4], BF),
    "zu": ("sbuf", [128, 33, 64], BF),
    "wt": ("sbuf", [128, 4 * TC], BF),
    "ones": ("sbuf", [128, 128], BF),
    "unit": ("sbuf", [128, 528], BF),
    "pidx": ("sbuf", [128, 2], I32),
    "pint": ("sbuf", [128, 4], I32),
    "pflt": ("sbuf", [128, 4], F32),
    "bas0": ("sbuf", [128, 128], I32),
    "bas": ("sbuf", [128, 128], I32),
    "xq": ("sbuf", [128, TC], X4), "xs": ("sbuf", [128, TC], "uint8"),
    "xq1": ("sbuf", [128, TC], X4), "xs1": ("sbuf", [128, TC], "uint8"),
    "zq": ("sbuf", [128, 528], X4), "zs": ("sbuf", [128, 528], "uint8"),
    "eq": ("sbuf", [128, 512], X4), "es": ("sbuf", [128, 512], "uint8"),
    "wq": ("sbuf", [128, 512], X4), "ws": ("sbuf", [128, 512], "uint8"),
    "hq": ("sbuf", [128, 2 * HAL], X4), "hs": ("sbuf", [128, 2 * HAL], "uint8"),
    "vw": ("sbuf", [128, 4 * WIN], F32),
    "dw": ("sbuf", [128, 4 * WIN], F32),
    "yb": ("sbuf", [128, 2 * TC], F32),
    "ps": ("psum", [128, 4096], F32),
}
for _k in range(2):
    SCRATCH.update({
        "ni%d" % _k: ("sbuf", [128, 128], I32), "pl%d" % _k: ("sbuf", [128, 128], I32),
        "wr%d" % _k: ("sbuf", [128, 32], I32), "ab%d" % _k: ("sbuf", [128, 128], F32),
        "sg%d" % _k: ("sbuf", [128, 128], F32), "dp%d" % _k: ("sbuf", [128, 128], I32),
        "vl%d" % _k: ("sbuf", [128, 128], U16), "dl%d" % _k: ("sbuf", [128, 128], U16),
        "tm%d" % _k: ("sbuf", [128, TC], F32), "rn%d" % _k: ("sbuf", [128, TC], F32),
        "fr%d" % _k: ("sbuf", [128, 4 * TC], F32), "pp%d" % _k: ("sbuf", [128, 4 * TC], F32),
        "mt%d" % _k: ("sbuf", [128, 4 * TC], BF),
        "mq%d" % _k: ("sbuf", [128, TC], X4), "ms%d" % _k: ("sbuf", [128, TC], "uint8"),
    })
SEMAPHORES = ["cV", "cS", "cP", "cG", "sent", "arrR", "arrL", "dx1", "dx2", "du", "dwt"] + \
    ["dy%d" % i for i in range(6)] + ["da%d" % i for i in range(4)]

Op, Fn = AluOpType, ActivationFunctionType


def scheduler(g, T):
    queues = {"V": g.vector, "S": g.scalar, "P": g.tensor, "G": g, "Y": g.sync}
    clock = {q: {} for q in queues}
    done = {}
    tick, log, scale = {}, {}, {}

    def after(q, reads, writes):
        deps = {}
        for acc, mine in ((reads, "r"), (writes, "w")):
            for key, lo, hi in acc:
                for (l, h, kind, src, t, oq) in log.get(key, []):
                    if h <= lo or hi <= l:
                        continue
                    bank = key[:2] == "ps"
                    if mine == "r" and kind == "r" and not (bank and oq != q):
                        continue
                    if src == "c" + q and (kind == "r" or bank):
                        continue
                    deps[src] = max(deps.get(src, 0), t)
        for src, t in list(deps.items()):
            if clock[q].get(src, 0) >= t:
                continue
            if any(s2 != src and done[(s2, t2)].get(src, 0) >= t and clock[q].get(s2, 0) < t2 for s2, t2 in deps.items()):
                continue
            queues[q].wait_ge(T.sem[src], t * scale.get(src, 1))
        for src, t in deps.items():
            for s, v in done[(src, t)].items():
                clock[q][s] = max(clock[q].get(s, 0), v)

    def note(q, src, reads, writes):
        tick[src] = tick.get(src, 0) + 1
        c = dict(clock[q]) if q else {}
        c[src] = tick[src]
        done[(src, tick[src])] = c
        for acc, kind in ((reads, "r"), (writes, "w")):
            for key, lo, hi in acc:
                log.setdefault(key, []).append((lo, hi, kind, src, tick[src], q))

    def do(q, call, reads, writes):
        after(q, reads, writes)
        call(queues[q]).then_inc(T.sem["c" + q], 1)
        note(q, "c" + q, reads, writes)

    def dma(q, sem, out, in_, reads, writes, **kw):
        after(q, reads, writes)
        queues[q].dma_start(out, in_, **kw).then_inc(T.sem[sem], 16)
        scale[sem] = 16
        note(q, sem, reads, writes)

    def arrival(sem, count, writes):
        scale[sem] = count
        note(None, sem, [], writes)

    def drain(q):
        for src, t in tick.items():
            if clock[q].get(src, 0) < t:
                queues[q].wait_ge(T.sem[src], t * scale.get(src, 1))

    return do, dma, after, arrival, drain


def rank_program(g, core, T, topo):
    rank = T.rank_of(core)
    if rank is None:
        return
    do, dma, after, arrival, drain = scheduler(g, T)
    prev = T.cores[rank - 1] if rank > 0 else None
    nxt = T.cores[rank + 1] if rank < N - 1 else None
    ENG = 4
    if nxt is not None:
        arrival("arrR", 2 * ENG, [("hq", 0, HAL)])
    if prev is not None:
        arrival("arrL", 2 * ENG, [("hq", HAL, 2 * HAL)])

    def quant(codes, planes, buf, c0, n, e0, lo, hi):
        do("V", lambda v: v.quantize_mx(T[codes][:, c0:c0 + n], T[planes][:, c0:c0 + n], T[buf][:, e0:e0 + 4 * n]),
           [(buf, lo, hi)], [(codes, c0, c0 + n)])

    names = {"zq": "zs", "xq": "xs", "xq1": "xs1", "eq": "es", "wq": "ws", "hq": "hs", "mq0": "ms0", "mq1": "ms1"}

    def mm(bank, n, ls, l0, rs, r0, start, stop):
        do("P", lambda p: p.matmul_mx(T.ps[:, 512 * bank:512 * bank + n], T[ls][:, l0:l0 + 128], T[names[ls]][:, l0:l0 + 128],
                                      T[rs][:, r0:r0 + n], T[names[rs]][:, r0:r0 + n], start, stop),
           [(ls, l0, l0 + 128), (rs, r0, r0 + n)], [("ps%d" % bank, 0, 512)])

    dma("Y", "dx1", T.xt[:, 0:1024], T.x[:, 0:1024], [], [("xt", 0, 256)])
    dma("S", "du", T.us[:, :, :], T.u[:, 0:64], [], [("us", 0, 1)])
    dma("Y", "dx2", T.xt[:, 1024:2048], T.x[:, 1024:2048], [], [("xt", 256, 512)])

    do("G", lambda e: e.iota(T.pidx[:, 0:1], [[0, 1]], 0, 1), [], [("pidx", 0, 1)])
    do("G", lambda e: e.iota(T.bas0[:], [[4, 128]], OWN, 0), [], [("bas0", 0, 1)])
    do("V", lambda v: v.memset(T.ones[:], 1.0), [], [("ones", 0, 1)])
    do("V", lambda v: v.memset(T.unit[:], 0.0), [], [("unit", 0, 1)])
    do("G", lambda e: e.affine_select(T.unit[:, 3:515:4], T.ones[:], [[-1, 128]], Op.is_equal, 0.0, 0, 1),
       [("ones", 0, 1)], [("unit", 0, 1)])
    do("V", lambda v: v.memset(T.zu[:, 0:17, :], 0.0), [], [("zuz", 0, 1)])
    do("V", lambda v: v.memset(T.xt[:, 2048:2064], 0.0), [], [("xt", 512, 516)])
    do("V", lambda v: v.memset(T.vw[:, 0:8], 0.0), [], [("vw%d" % b, 0, 2) for b in range(4)])
    do("V", lambda v: v.memset(T.dw[:, 0:8], 0.0), [], [("dw%d" % b, 0, 2) for b in range(4)])
    if nxt is None:
        for w, lo in (("dw", RGT - 1), ("vw", RGT)):
            do("G", lambda e: e.iota(T[w][:, 4 * lo:4 * LFT], [[0, 4 * (LFT - lo)]], 0, 0, allow_small_or_imprecise_dtypes=True),
               [], [("%s%d" % (w, b), lo, LFT) for b in range(4)])
    do("V", lambda v: v.tensor_scalar(T.pint[:, 0:1], T.pidx[:, 0:1], 3, None, Op.bitwise_and), [("pidx", 0, 1)], [("pint", 0, 1)])
    do("V", lambda v: v.tensor_scalar(T.pint[:, 1:2], T.pidx[:, 0:1], 2, 3, Op.arith_shift_right, Op.bitwise_and),
       [("pidx", 0, 1)], [("pint", 1, 2)])
    do("V", lambda v: v.tensor_copy(T.pflt[:, 0:2], T.pint[:, 0:2]), [("pint", 0, 2)], [("pflt", 0, 1)])
    do("V", lambda v: v.tensor_scalar(T.bas[:], T.bas0[:], T.pflt[:, 1:2], None, Op.add), [("bas0", 0, 1), ("pflt", 0, 1)], [("bas", 0, 1)])

    def unit_q(b):
        quant("eq", "es", "unit", 128 * b, 128, 3 - b, 0, 1)

    unit_q(0); unit_q(1)

    us = [("us", 0, 1)]
    do("V", lambda v: v.tensor_copy(T.zu[:, 0:16, 48:52], T.us[:, :, :]), us, [("zuz", 0, 1)])
    do("V", lambda v: v.tensor_copy(T.zu[:, 0:16, 52:56], T.us[:, :, :]), us, [("zuz", 0, 1)])
    do("S", lambda s: s.activation(T.zu[:, 17:33, 0:4], T.us[:, :, :], Fn.Copy), us, [("zuu", 0, 4)])
    do("S", lambda s: s.activation(T.zu[:, 17:33, 4:8], T.us[:, :, :], Fn.Copy), us, [("zuu", 4, 8)])
    do("V", lambda v: v.tensor_copy(T.zu[:, 0:16, 56:64], T.zu[:, 0:16, 48:56]), [("zuz", 0, 1)], [("zuz", 0, 1)])
    for w in (8, 16, 32):
        do("S", lambda s: s.activation(T.zu[:, 17:33, w:2 * w], T.zu[:, 17:33, 0:w], Fn.Copy), [("zuu", 0, w)], [("zuu", w, 2 * w)])
    do("V", lambda v: v.quantize_mx(T.zq[:, 0:272], T.zs[:, 0:272], T.zu[:, 0:17, :]), [("zuz", 0, 1)], [("zq", 0, 272)])

    quant("xq", "xs", "xt", 0, 256, 0, 0, 256)
    quant("xq", "xs", "xt", 256, 256, 1024, 256, 512)
    quant("xq1", "xs1", "xt", 0, 254, 4, 1, 255)
    quant("xq1", "xs1", "xt", 254, 258, 1020, 255, 513)
    do("V", lambda v: v.quantize_mx(T.zq[:, 272:528], T.zs[:, 272:528], T.zu[:, 17:33, :]), [("zuu", 0, 64)], [("zq", 272, 528)])

    sends = []
    if prev is not None:
        sends.append((prev, 0, 0, "arrR"))
    if nxt is not None:
        sends.append((nxt, TC - HAL, HAL, "arrL"))
    after("G", [("xq", c0, c0 + HAL) for _, c0, _, _ in sends], [])
    for plane in (0, 1):
        tr = []
        for i, (dst, c0, d0, sem) in enumerate(sends):
            rid, pid, _ = topo.addr(dst)
            eng = topo.engines(core, dst)[ENG * i:ENG * i + ENG]
            s, d = (T.xs[:, c0:c0 + HAL], T.hs[:, d0:d0 + HAL]) if plane else \
                (T.xq[:, c0:c0 + HAL].bitcast(dt.uint8), T.hq[:, d0:d0 + HAL].bitcast(dt.uint8))
            tr.append(RemoteDMATransfer(dst_ids=[DstId(rid=rid, pnc=pid)], dma_engine_mask=sum(1 << e for e in eng),
                                        remote_sem=T.sem[sem], src=s, dst=d))
        g.remote_dma_fused(tr, local_sem=T.sem.sent)
    sent = 2 * ENG * len(sends)

    after("Y", [("xt", 0, 512)], [])
    dma("Y", "dwt", T.wt[:], T.w[:], [], [("wt", 0, 1)])

    def unpack_mm(b):
        mm(b, TC, "eq", 128 * b, "xq", 0, True, True)

    def unpack_copy(b):
        do("S", lambda s: s.activation(T.vw[:, 4 * OWN + b:4 * RGT:4], T.ps[:, 512 * b:512 * b + 512], Fn.Copy),
           [("ps%d" % b, 0, 512)], [("vw%d" % b, OWN, RGT)])

    def diff(b):
        do("V", lambda v: v.tensor_tensor(T.dw[:, 4 * OWN + b:4 * (RGT - 1):4], T.ps[:, 512 * b + 1:512 * b + 512],
                                          T.vw[:, 4 * OWN + b:4 * (RGT - 1):4], Op.subtract),
           [("ps%d" % b, 0, 512), ("vw%d" % b, OWN, RGT - 1)], [("dw%d" % b, OWN, RGT - 1)])

    def offs_mm(k):
        mm(6 + k, TC, "zq", 272 + 128 * k, "xq", 0, True, True)

    def list_mm(k):
        for n, a in enumerate((0, 2, 1, 3)):
            mm(4 + k, 510, "zq", 128 * k + 12 - 4 * a, "xq1" if a % 2 else "xq", a - a % 2, n == 0, n == 3)

    def frac_n(k, j0, j1):
        do("S", lambda s: s.activation(T["tm%d" % k][:, j0:j1], T.ps[:, 512 * (6 + k) + j0:512 * (6 + k) + j1], Fn.Copy, bias=MAGIC),
           [("ps%d" % (6 + k), 0, 512)], [("tm%d" % k, j0, j1)])
        do("S", lambda s: s.activation(T["rn%d" % k][:, j0:j1], T["tm%d" % k][:, j0:j1], Fn.Copy, bias=-MAGIC),
           [("tm%d" % k, j0, j1)], [("rn%d" % k, j0, j1)])

    def frac_sub(k, j0, j1):
        do("V", lambda v: v.tensor_tensor(T["fr%d" % k][:, 4 * j0:4 * j1:4], T.ps[:, 512 * (6 + k) + j0:512 * (6 + k) + j1],
                                          T["rn%d" % k][:, j0:j1], Op.subtract),
           [("ps%d" % (6 + k), 0, 512), ("rn%d" % k, j0, j1)], [("fr%d0" % k, j0, j1)])

    def frac_rep(q, k, j0, j1, bs):
        for b in bs:
            out, in_ = T["fr%d" % k][:, 4 * j0 + b:4 * j1:4], T["fr%d" % k][:, 4 * j0:4 * j1:4]
            call = {"S": lambda s: s.activation(out, in_, Fn.Copy), "V": lambda v: v.tensor_copy(out, in_),
                    "G": lambda e: e.affine_select(out, in_, [[1, j1 - j0]], Op.is_gt, 0.0, 1, 0)}[q]
            do(q, call, [("fr%d0" % k, j0, j1)], [("fr%d%d" % (k, b), j0, j1)])

    def inside(k):
        ab, sg = T["ab%d" % k], T["sg%d" % k]
        do("S", lambda s: s.activation(ab[:], T.ps[:, 512 * (4 + k):512 * (4 + k) + 509:4], Fn.Abs), [("ps%d" % (4 + k), 0, 512)], [("ab%d" % k, 0, 128)])
        do("S", lambda s: s.activation(sg[:], ab[:], Fn.Sign, bias=float(CL), scale=-1.0), [("ab%d" % k, 0, 128)], [("sg%d" % k, 0, 128)])

    def lists(k):
        ni, pl, wr, sg, dp, vl, dl = (T[n + str(k)] for n in ("ni", "pl", "wr", "sg", "dp", "vl", "dl"))
        key = lambda n, lo=0, hi=128: (n + str(k), lo, hi)
        d = T.ps[:, 512 * (4 + k):512 * (4 + k) + 509:4]
        do("V", lambda v: v.tensor_scalar(ni[:], d, float(-CL), float(CL), Op.max, Op.min), [("ps%d" % (4 + k), 0, 512)], [key("ni")])
        do("V", lambda v: v.tensor_tensor(pl[:], ni[:], T.bas[:], Op.add), [key("ni"), ("bas", 0, 1)], [key("pl")])
        if prev is None:
            do("V", lambda v: v.tensor_scalar(pl[:, 0:32], pl[:, 0:32], float(OWN), None, Op.max), [key("pl", 0, 32)], [key("pl", 0, 32)])
        else:
            do("V", lambda v: v.tensor_scalar(wr[:], pl[:, 0:32], float(OWN), float(WIN - OWN), Op.is_lt, Op.mult), [key("pl", 0, 32)], [key("wr")])
            do("V", lambda v: v.tensor_tensor(pl[:, 0:32], pl[:, 0:32], wr[:], Op.add), [key("pl", 0, 32), key("wr")], [key("pl", 0, 32)])
        if nxt is None:
            do("V", lambda v: v.tensor_scalar(pl[:, 96:128], pl[:, 96:128], float(RGT - 1), None, Op.min), [key("pl", 96, 128)], [key("pl", 96, 128)])
        do("V", lambda v: v.tensor_scalar(vl[:], pl[:], 4.0, T.pflt[:, 0:1], Op.mult, Op.add), [key("pl"), ("pflt", 0, 1)], [key("vl")])
        do("V", lambda v: v.tensor_tensor(dp[:], pl[:], sg[:], Op.mult), [key("pl"), key("sg")], [key("dp")])
        do("V", lambda v: v.tensor_scalar(dl[:], dp[:], 4.0, T.pflt[:, 0:1], Op.mult, Op.add), [key("dp"), ("pflt", 0, 1)], [key("dl")])

    def slope(k, j0, j1, end):
        do("V", lambda v: v.tensor_tensor(T["pp%d" % k][:, 4 * j0:4 * j1], T.dw[:, 0:4 * end].indirect(T["dl%d" % k][:, j0 // 4:j1 // 4]),
                                          T["fr%d" % k][:, 4 * j0:4 * j1], Op.mult),
           [("dw%d" % b, 0, end) for b in range(4)] + [("fr%d%d" % (k, b), j0, j1) for b in range(4)] + [("dl%d" % k, 0, 128)],
           [("pp%d" % k, j0, j1)])

    def tap(k, j0, j1, end):
        do("V", lambda v: v.tensor_tensor(T["mt%d" % k][:, 4 * j0:4 * j1], T.vw[:, 0:4 * end].indirect(T["vl%d" % k][:, j0 // 4:j1 // 4]),
                                          T["pp%d" % k][:, 4 * j0:4 * j1], Op.add),
           [("vw%d" % b, 0, end) for b in range(4)] + [("pp%d" % k, j0, j1), ("vl%d" % k, 0, 128)], [("mt%d" % k, j0, j1)])

    def far_v(k, j0, j1, end):
        do("S", lambda s: s.activation(T["mt%d" % k][:, 4 * j0:4 * j1], T.vw[:, 0:4 * end].indirect(T["vl%d" % k][:, j0 // 4:j1 // 4]), Fn.Copy),
           [("vw%d" % b, 0, end) for b in range(4)] + [("vl%d" % k, 0, 128)], [("mt%d" % k, j0, j1)])

    def far_add(k, j0, j1, sem):
        dma("G", sem, T["mt%d" % k][:, 4 * j0:4 * j1], T["pp%d" % k][:, 4 * j0:4 * j1],
            [("pp%d" % k, j0, j1), ("mt%d" % k, j0, j1)], [("mt%d" % k, j0, j1)], accum_op=Op.add)

    def finish(j0, j1, banks, n, first=0, last=False):
        for k in (first, 1 - first):
            quant("mq%d" % k, "ms%d" % k, "mt%d" % k, j0, j1 - j0, 4 * j0, j0, j1)
            for o in range(2):
                mm(banks[o], j1 - j0, "wq", 128 * (2 * k + o), "mq%d" % k, j0, k == first, k != first)
        for o in range(2):
            src, dst = T.ps[:, 512 * banks[o]:512 * banks[o] + j1 - j0], T.yb[:, TC * o + j0:TC * o + j1]
            acc = ([("ps%d" % banks[o], 0, 512)], [("yb%d" % o, j0, j1)])
            if last and o == 1:
                do("V", lambda v: v.tensor_copy(dst, src), *acc)
            else:
                do("S", lambda s: s.activation(dst, src, Fn.Copy), *acc)
            dma("S" if last and o == 1 else "Y", "dy%d" % (2 * n + o), T.y[:, TC * o + j0:TC * o + j1], dst, [("yb%d" % o, j0, j1)], [])

    A, LO, HI = (128, 384), (0, 128), (384, 512)
    unpack_mm(0); unpack_mm(1); offs_mm(0); list_mm(0)
    unpack_copy(0); unpack_copy(1)
    frac_n(0, *A); frac_n(0, *LO); frac_n(0, *HI)
    diff(0); diff(1); frac_sub(0, *A); frac_rep("S", 0, *A, (1, 2)); frac_rep("V", 0, *A, (3,))
    unit_q(2); unit_q(3)
    unpack_mm(2); unpack_mm(3); offs_mm(1); list_mm(1)
    frac_sub(0, *LO); frac_sub(0, *HI); frac_rep("G", 0, *LO, (2, 3)); frac_rep("G", 0, *HI, (2, 3))
    inside(0); unpack_copy(2); unpack_copy(3); lists(0)
    diff(2); diff(3)
    frac_n(1, 0, TC)
    slope(0, *A, RGT - 1)
    far_v(0, *A, RGT)
    frac_sub(1, 0, TC)
    inside(1)
    frac_rep("G", 1, *A, (3,)); frac_rep("S", 1, *A, (1, 2))
    far_add(0, *A, "da0")
    frac_rep("G", 1, *LO, (3,)); frac_rep("G", 1, *HI, (3,))
    lists(1)
    slope(1, *A, RGT - 1)
    far_v(1, *A, RGT); far_add(1, *A, "da1")

    h0, h1 = (0 if nxt is not None else HAL), (2 * HAL if prev is not None else HAL)
    w0, w1 = RGT + h0, RGT + h1
    e = 1 if nxt is None else 0
    for b in range(4):
        mm(b, h1 - h0, "eq", 128 * b, "hq", h0, True, True)
    for b in range(4):
        do("S", lambda s: s.activation(T.vw[:, 4 * w0 + b:4 * w1:4], T.ps[:, 512 * b:512 * b + w1 - w0], Fn.Copy),
           [("ps%d" % b, 0, 512)], [("vw%d" % b, w0, w1)])
        do("V", lambda v: v.tensor_tensor(T.dw[:, 4 * (w0 - 1 + e) + b:4 * (w1 - 1):4], T.ps[:, 512 * b + e:512 * b + w1 - w0],
                                          T.vw[:, 4 * (w0 - 1 + e) + b:4 * (w1 - 1):4], Op.subtract),
           [("ps%d" % b, 0, 512), ("vw%d" % b, w0 - 1 + e, w1 - 1)], [("dw%d" % b, w0 - 1 + e, w1 - 1)])
    if prev is not None:
        do("V", lambda v: v.tensor_tensor(T.dw[:, 4 * (WIN - 1):4 * WIN], T.vw[:, 4 * OWN:4 * OWN + 4], T.vw[:, 4 * (WIN - 1):4 * WIN], Op.subtract),
           [("vw%d" % b, OWN, OWN + 1) for b in range(4)] + [("vw%d" % b, WIN - 1, WIN) for b in range(4)],
           [("dw%d" % b, WIN - 1, WIN) for b in range(4)])
    frac_rep("S", 0, *LO, (1,)); frac_rep("S", 0, *HI, (1,)); frac_rep("S", 1, *LO, (1, 2)); frac_rep("S", 1, *HI, (1, 2))

    L = LO + ((RGT - 1, RGT) if prev is None else (WIN, WIN))
    R = HI + ((LFT - 1, LFT) if nxt is not None else (RGT, RGT))
    E1, E2 = (L, R) if prev is None else (R, L)
    slope(0, *E1[:3]); far_v(0, *E1[:2], E1[3]); far_add(0, *E1[:2], "da2")
    slope(0, *E2[:3]); far_v(0, *E2[:2], E2[3]); far_add(0, *E2[:2], "da3")
    slope(1, *E1[:3]); slope(1, *E2[:3])
    tap(1, *E1[:2], E1[3])
    quant("wq", "ws", "wt", 0, 512, 0, 0, 1)
    finish(*A, (4, 5), 0)
    finish(*E1[:2], (6, 7), 1)
    tap(1, *E2[:2], E2[3])
    finish(*E2[:2], (0, 1), 2, first=1, last=True)
    g.wait_ge(T.sem.sent, sent)
    drain("Y")
